import numpy as np
import ml_dtypes


def mxq(x, axis, fmt="e4m3"):
    dtype, down = {"e4m3": (ml_dtypes.float8_e4m3fn, 7), "e5m2": (ml_dtypes.float8_e5m2, 14)}[fmt]
    v = np.moveaxis(np.asarray(x, np.float32).astype(ml_dtypes.bfloat16).astype(np.float64), axis, -1)
    blocks = v.reshape(v.shape[:-1] + (-1, 32))
    amax = np.abs(blocks).max(-1, keepdims=True)
    byte = np.maximum(np.where(amax > 0, np.frexp(amax)[1] - 1 + 127, 0) - down, 1)
    scale = np.exp2(byte - 127.0)
    codes = (blocks / scale).astype(np.float32).astype(dtype).astype(np.float64)
    return np.moveaxis((codes * scale).reshape(v.shape), -1, axis)


WIDE = False


def mx_kscale(k):
    if not WIDE:
        return np.ones(k)
    levels = np.array([10, -10, 5, -5, 0])
    if k % 512:
        return np.exp2(np.random.permutation(np.resize(levels, k // 32))).repeat(32)
    a = np.empty((k // 512, 16))
    for p in range(k // 512):
        a[p, :8] = np.random.permutation(np.resize(levels, 8))
        for g in range(8):
            far = levels[np.abs(levels - a[p, g]) >= 10]
            a[p, g + 8] = far[np.random.randint(len(far))]
    return np.exp2(a.ravel()).repeat(32)


def f64(x):
    return np.asarray(x).astype(np.float64)


def striped(idx):
    return np.tile(np.asarray(idx).reshape(-1, 16).T, (8, 1)).astype(np.uint16)


def unstriped(offs):
    return offs[:16].T.reshape(-1).astype(np.int64)


def striped8(idx):
    return np.asarray(idx).reshape(8, -1, 16).transpose(0, 2, 1).reshape(128, -1).astype(np.uint16)


def unstriped8(offs):
    return offs.reshape(8, 16, -1).transpose(0, 2, 1).reshape(8, -1).astype(np.int64)


def pick8(x, idx, run):
    r = np.arange(len(x))
    return x[r[:, None], idx[r % (8 * run) // run]]


E2M1 = np.array([0.0, 0.5, 1.0, 1.5, 2.0, 3.0, 4.0, 6.0, -0.0, -0.5, -1.0, -1.5, -2.0, -3.0, -4.0, -6.0])


def pack_weight(w, fmt):
    k, n = w.shape
    w = f64(np.asarray(w, np.float32).astype(ml_dtypes.bfloat16)).reshape(k // 32, 32, n)
    amax = np.abs(w).max(1)
    if fmt == "e4m3":
        byte = np.frexp(amax)[1] - 1 + 127 - 7
    else:
        mant, ex = np.frexp(amax / 6.0)
        byte = np.where(mant > 0.5, ex, ex - 1) + 127
    byte = np.clip(np.where(amax > 0, byte, 1), 1, 254)
    scaled = (w * np.exp2(127.0 - byte)[:, None, :]).reshape(k, n).astype(np.float32)
    by_word = np.ascontiguousarray(scaled.reshape(k // 512, 128, 4, n).transpose(0, 1, 3, 2))
    if fmt == "e4m3":
        words = by_word.astype(ml_dtypes.float8_e4m3fn).view(np.uint8)
    else:
        c = by_word.astype(ml_dtypes.float4_e2m1fn).view(np.uint8) & 0xF
        words = (c[..., 0::2] | (c[..., 1::2] << 4)).reshape(k // 512, 128, 2 * n)
    return np.ascontiguousarray(words), np.ascontiguousarray(byte.astype(np.uint8).reshape(k // 512, 16, n))


def unpack_weight(words, scales, fmt):
    g, _, n = scales.shape
    words = np.ascontiguousarray(words).reshape(g, 128, n, -1)
    if fmt == "e4m3":
        vals = words.view(ml_dtypes.float8_e4m3fn).astype(np.float64)
    else:
        nib = np.empty((g, 128, n, 4), np.uint8)
        nib[..., 0::2] = words & 0xF
        nib[..., 1::2] = words >> 4
        vals = E2M1[nib]
    vals = vals * np.repeat(np.exp2(scales.astype(np.float64) - 127.0), 8, axis=1)[..., None]
    return vals.transpose(0, 1, 3, 2).reshape(g * 512, n)


K, J, R, T, F, O, C, N = 512, 512, 512, 2048, 1024, 192, 256, 256


def setup_inputs():
    n = np.random.standard_normal
    idx = np.random.permutation(T)[:J]
    idx2 = np.random.permutation(F)[:R]
    idx3 = np.stack([np.random.permutation(J)[:O] for _ in range(8)])
    idx4 = np.stack([np.random.permutation(C)[:O] for _ in range(8)])
    idx5 = np.stack([np.random.permutation(J)[:C] for _ in range(8)])
    idx6 = np.random.permutation(T)[:C]
    fk = mx_kscale(K)
    fr = mx_kscale(R)
    tr = np.ones(F)
    tr[idx2] = fr
    xtp = pack_weight(n((K, T)) * fk[:, None], "e4m3")
    wtp = pack_weight(n((K, F)) * 1 / np.sqrt(K) / fk[:, None] * tr, "e4m3")
    wbp = pack_weight(n((R, N)) * 1 / np.sqrt(R) / fr[:, None], "e2m1")
    wsp = pack_weight(n((K, N)) * 1 / np.sqrt(K) / fk[:, None], "e2m1")
    return {
        "xt_words": xtp[0],
        "xt_scales": xtp[1],
        "wt_words": wtp[0],
        "wt_scales": wtp[1],
        "sa": (np.random.uniform(0.5, 1.6, (R, 1))).astype(np.float32),
        "sb": (np.random.uniform(0.5, 1.6, (R, 1))).astype(np.float32),
        "wb_words": wbp[0],
        "wb_scales": wbp[1],
        "ws_words": wsp[0],
        "ws_scales": wsp[1],
        "offs": striped(idx),
        "offs2": striped(idx2),
        "offs3": striped8(idx3),
        "offs4": striped8(idx4),
        "offs5": striped8(idx5),
        "offs6": striped(idx6),
    }


def reference(xt_words, xt_scales, wt_words, wt_scales, sa, sb, wb_words, wb_scales, ws_words, ws_scales, offs, offs2, offs3, offs4, offs5, offs6):
    idx = unstriped(offs)
    idx2 = unstriped(offs2)
    idx3 = unstriped8(offs3)
    idx4 = unstriped8(offs4)
    idx5 = unstriped8(offs5)
    idx6 = unstriped(offs6)
    xtu = unpack_weight(xt_words, xt_scales, "e4m3")
    wtu = unpack_weight(wt_words, wt_scales, "e4m3")
    wbu = unpack_weight(wb_words, wb_scales, "e2m1")
    wsu = unpack_weight(ws_words, ws_scales, "e2m1")
    wtidx2g = wtu[:, idx2]
    xtidxg = xtu[:, idx]
    a = wtidx2g.T @ xtidxg
    h1 = pick8(a, idx3, 64) * f64(sa)
    pw = np.zeros((R, C))
    pw[np.arange(R)[:, None], idx4[np.arange(R) % 512 // 64]] = h1
    hid = np.abs(pw - pick8(a, idx5, 64) * f64(sb))
    hidq = mxq(hid, 0, "e4m3")
    xtidx6g = xtu[:, idx6]
    y = wbu.T @ hidq + wsu.T @ xtidx6g
    return y

@@ -1,0 +1,202 @@
+from contextlib import ExitStack
+
+import concourse.mybir as mybir
+
+K, J, R, T, F, O, C, N = 512, 512, 512, 2048, 1024, 192, 256, 256
+FLOPS = 2 * K * R * J + 2 * R * N * C + 2 * K * N * C
+
+F32 = mybir.dt.float32
+BF16 = mybir.dt.bfloat16
+I32 = mybir.dt.int32
+U32 = mybir.dt.uint32
+U16 = mybir.dt.uint16
+U8 = mybir.dt.uint8
+FP8X4 = mybir.dt.float8_e4m3fn_x4
+FP4X4 = mybir.dt.float4_e2m1fn_x4
+COPY = mybir.ActivationFunctionType.Copy
+ALU = mybir.AluOpType
+
+P = 128
+PACK = 4
+LIST_ROWS = 16
+HALF_J = J // 2
+HALF_C = C // 2
+
+
+def load_scale_rows(queue, plane, scales):
+    for q in range(4):
+        queue.dma_start(out=plane[32 * q : 32 * q + 4, :].bitcast(I32), in_=scales[0, 4 * q : 4 * q + 4, :].bitcast(I32))
+
+
+def entries(offsets, first, count):
+    return offsets[:, first // LIST_ROWS : (first + count) // LIST_ROWS]
+
+
+def tile_picked_tokens_store_one_wholepage_further_plain_kernel(
+    tc, xt_words, xt_scales, wt_words, wt_scales, sa, sb, wb_words, wb_scales, ws_words, ws_scales,
+    offs, offs2, offs3, offs4, offs5, offs6, out,
+):
+    nc = tc.nc
+    with ExitStack() as ctx:
+        keep = ctx.enter_context(tc.tile_pool(name="keep", bufs=1))
+        psum = ctx.enter_context(tc.psum_pool(name="psum", bufs=1))
+
+        slot_list = keep.tile([P, J // LIST_ROWS], U16)
+        feature_list = keep.tile([P, R // LIST_ROWS], U16)
+        fill_from = keep.tile([P, O // LIST_ROWS], U16)
+        fill_to = keep.tile([P, O // LIST_ROWS], U16)
+        page_list = keep.tile([P, C // LIST_ROWS], U16)
+        short_list = keep.tile([P, C // LIST_ROWS], U16)
+
+        xt_w = keep.tile([P, T], U32, align_bytes=64)
+        xt_s = keep.tile([P, T], U8, align_bytes=64)
+        wt_w = keep.tile([P, F], U32, align_bytes=64)
+        wt_s = keep.tile([P, F], U8, align_bytes=64)
+        wb_w = keep.tile([P, 2 * N], U8, align_bytes=64)
+        wb_s = keep.tile([P, N], U8, align_bytes=64)
+        ws_w = keep.tile([P, 2 * N], U8, align_bytes=64)
+        ws_s = keep.tile([P, N], U8, align_bytes=64)
+        sa_t = keep.tile([P, PACK], F32)
+        sb_t = keep.tile([P, PACK], F32)
+        pages = [keep.tile([P, C], F32, name=f"page{t}") for t in range(PACK)]
+
+        for plane in (wt_s, xt_s, ws_s, wb_s):
+            nc.vector.memset(plane[:].bitcast(I32), 0)
+        for page in pages:
+            nc.vector.memset(page[:], 0.0)
+
+        nc.sync.dma_start(feature_list[:], offs2)
+        nc.sync.dma_start(slot_list[:], offs)
+        load_scale_rows(nc.scalar, wt_s, wt_scales)
+        nc.sync.dma_start(out=wt_w[:].bitcast(I32), in_=wt_words[0].rearrange("p n t -> p (n t)").bitcast(I32))
+        nc.sync.dma_start(out=xt_w[:].bitcast(I32), in_=xt_words[0].rearrange("p n t -> p (n t)").bitcast(I32))
+        load_scale_rows(nc.scalar, xt_s, xt_scales)
+        nc.sync.dma_start(fill_from[:], offs3)
+        nc.sync.dma_start(out=sa_t[:], in_=sa.rearrange("(p t) o -> p (t o)", t=PACK))
+        nc.sync.dma_start(fill_to[:], offs4)
+        nc.sync.dma_start(page_list[:], offs5)
+        nc.sync.dma_start(out=sb_t[:], in_=sb.rearrange("(p t) o -> p (t o)", t=PACK))
+        nc.sync.dma_start(short_list[:], offs6)
+        nc.sync.dma_start(out=ws_w[:].bitcast(I32), in_=ws_words[0].bitcast(I32))
+        nc.sync.dma_start(out=wb_w[:].bitcast(I32), in_=wb_words[0].bitcast(I32))
+        load_scale_rows(nc.sync, ws_s, ws_scales)
+        load_scale_rows(nc.sync, wb_s, wb_scales)
+
+        feat_s = keep.tile([P, R], U8, align_bytes=64)
+        feat_w = keep.tile([P, R], U32, align_bytes=64)
+        slot_s = keep.tile([P, J], U8, align_bytes=64)
+        slot_w = [keep.tile([P, HALF_J], U32, align_bytes=64, name=f"slot_w{h}") for h in range(2)]
+        nc.vector.tensor_copy(feat_s[:].rearrange("p (t m) -> p m t", t=PACK), wt_s[:].indirect(feature_list[:]))
+        nc.vector.tensor_copy(feat_w[:].rearrange("p (t m) -> p m t", t=PACK), wt_w[:].indirect(feature_list[:]))
+        nc.vector.tensor_copy(slot_s[:], xt_s[:].indirect(slot_list[:]))
+        for h in range(2):
+            nc.vector.tensor_copy(slot_w[h][:], xt_w[:].indirect(entries(slot_list, h * HALF_J, HALF_J)))
+
+        hidden = [keep.tile([P, J], F32, name=f"hidden{t}") for t in range(PACK)]
+
+        def first_product(acc, t, h):
+            nc.tensor.matmul_mx(
+                out=acc,
+                lhsT=feat_w[:, t * P : (t + 1) * P].bitcast(FP8X4),
+                lhsT_scale=feat_s[:, t * P : (t + 1) * P],
+                rhs=slot_w[h][:].bitcast(FP8X4),
+                rhs_scale=slot_s[:, h * HALF_J : (h + 1) * HALF_J],
+                start=True,
+                stop=True,
+            )
+
+        for h in range(2):
+            bank = psum.tile([P, HALF_J], F32, name=f"lead{h}", tag=f"lead{h}")
+            first_product(bank[:], 0, h)
+            nc.scalar.copy(hidden[0][:, h * HALF_J : (h + 1) * HALF_J], bank[:])
+        for t in range(1, PACK):
+            bank = psum.tile([P, J], F32, name=f"rest{t}", tag=f"rest{t}")
+            for h in range(2):
+                first_product(bank[:, h * HALF_J : (h + 1) * HALF_J], t, h)
+            nc.vector.tensor_copy(hidden[t][:], bank[:])
+
+        short_s = keep.tile([P, C], U8, align_bytes=64)
+        short_w = keep.tile([P, C], U32, align_bytes=64)
+        nc.vector.tensor_copy(short_s[:], xt_s[:].indirect(short_list[:]))
+        nc.vector.tensor_copy(short_w[:], xt_w[:].indirect(short_list[:]))
+
+        sums = {}
+        for h in range(2):
+            for nt in range(2):
+                tag = "lead0" if (h, nt) == (1, 1) else f"sum{h}{nt}"
+                sums[h, nt] = psum.tile([P, HALF_C], F32, name=f"sum{h}{nt}", tag=tag)
+                nc.tensor.matmul_mx(
+                    out=sums[h, nt][:],
+                    lhsT=ws_w[:, 2 * nt * P : 2 * (nt + 1) * P].bitcast(FP4X4),
+                    lhsT_scale=ws_s[:, nt * P : (nt + 1) * P],
+                    rhs=short_w[:, h * HALF_C : (h + 1) * HALF_C].bitcast(FP8X4),
+                    rhs_scale=short_s[:, h * HALF_C : (h + 1) * HALF_C],
+                    start=True,
+                    stop=False,
+                )
+
+        fetched = [keep.tile([P, C], F32, name=f"fetched{t}") for t in range(PACK)]
+        filling = [keep.tile([P, O], F32, name=f"filling{t}") for t in range(PACK)]
+        diff = [keep.tile([P, C], F32, name=f"diff{t}") for t in range(PACK)]
+        hid = [keep.tile([P, HALF_C, PACK], BF16, align_bytes=64, name=f"hid{h}") for h in range(2)]
+
+        def fetch_filling(t):
+            nc.scalar.activation(filling[t][:], hidden[t][:].indirect(fill_from[:]), COPY, scale=sa_t[:, t : t + 1])
+
+        def fill_page(t):
+            nc.scalar.activation(pages[t][:].indirect(fill_to[:]), filling[t][:], COPY)
+
+        def fetch_columns(t, first, count):
+            nc.scalar.activation(
+                fetched[t][:, first : first + count],
+                hidden[t][:].indirect(entries(page_list, first, count)),
+                COPY,
+                scale=sb_t[:, t : t + 1],
+            )
+
+        def magnitude(t, h):
+            cols = slice(h * HALF_C, (h + 1) * HALF_C)
+            nc.vector.tensor_tensor(diff[t][:, cols], pages[t][:, cols], fetched[t][:, cols], ALU.subtract)
+            nc.vector.scalar_tensor_tensor(hid[h][:, :, t], diff[t][:, cols], -1.0, diff[t][:, cols], ALU.mult, ALU.max)
+
+        def finish(h):
+            codes = keep.tile([P, HALF_C], U32, align_bytes=64, name=f"codes{h}")
+            scales = keep.tile([P, HALF_C], U8, align_bytes=64, name=f"scales{h}")
+            nc.vector.quantize_mx(out=codes[:].bitcast(FP8X4), scales=scales[:], in_=hid[h][:].rearrange("p c t -> p (c t)"))
+            for nt in range(2):
+                nc.tensor.matmul_mx(
+                    out=sums[h, nt][:],
+                    lhsT=wb_w[:, 2 * nt * P : 2 * (nt + 1) * P].bitcast(FP4X4),
+                    lhsT_scale=wb_s[:, nt * P : (nt + 1) * P],
+                    rhs=codes[:].bitcast(FP8X4),
+                    rhs_scale=scales[:],
+                    start=False,
+                    stop=True,
+                )
+            for nt in range(2):
+                result = keep.tile([P, HALF_C], F32, name=f"result{h}{nt}")
+                target = out[nt * P : (nt + 1) * P, h * HALF_C : (h + 1) * HALF_C]
+                if nt == 0:
+                    nc.scalar.copy(result[:], sums[h, nt][:])
+                    nc.scalar.dma_start(out=target, in_=result[:])
+                else:
+                    nc.vector.tensor_copy(result[:], sums[h, nt][:])
+                    nc.sync.dma_start(out=target, in_=result[:])
+
+        for t in range(2):
+            fetch_filling(t)
+            fetch_columns(t, 0, C)
+            fill_page(t)
+            magnitude(t, 0)
+            magnitude(t, 1)
+        for t in range(2, PACK):
+            fetch_filling(t)
+            fetch_columns(t, 0, HALF_C)
+            fill_page(t)
+            magnitude(t, 0)
+        for t in range(2, PACK):
+            fetch_columns(t, HALF_C, HALF_C)
+        finish(0)
+        for t in range(2, PACK):
+            magnitude(t, 1)
+        finish(1)

@@ -14,12 +14,13 @@ U8 = mybir.dt.uint8
 FP8X4 = mybir.dt.float8_e4m3fn_x4
 FP4X4 = mybir.dt.float4_e2m1fn_x4
 COPY = mybir.ActivationFunctionType.Copy
+ABS = mybir.ActivationFunctionType.Abs
 ALU = mybir.AluOpType
 
 P = 128
 PACK = 4
 LIST_ROWS = 16
-HALF_J = J // 2
+SLOT_PIECES = ((0, 256), (256, 128), (384, 128))
 HALF_C = C // 2
 
 
@@ -60,17 +61,21 @@ def tile_picked_tokens_store_one_wholepage_further_plain_kernel(
         sb_t = keep.tile([P, PACK], F32)
         pages = [keep.tile([P, C], F32, name=f"page{t}") for t in range(PACK)]
 
-        for plane in (wt_s, xt_s, ws_s, wb_s):
+        for plane in (wt_s, xt_s):
             nc.vector.memset(plane[:].bitcast(I32), 0)
         for page in pages:
             nc.vector.memset(page[:], 0.0)
+        for plane in (ws_s, wb_s):
+            nc.vector.memset(plane[:].bitcast(I32), 0)
 
+        xt_rows = xt_words[0].rearrange("p n t -> p (n t)").bitcast(I32)
         nc.sync.dma_start(feature_list[:], offs2)
+        load_scale_rows(nc.sync, wt_s, wt_scales)
         nc.sync.dma_start(slot_list[:], offs)
-        load_scale_rows(nc.scalar, wt_s, wt_scales)
         nc.sync.dma_start(out=wt_w[:].bitcast(I32), in_=wt_words[0].rearrange("p n t -> p (n t)").bitcast(I32))
-        nc.sync.dma_start(out=xt_w[:].bitcast(I32), in_=xt_words[0].rearrange("p n t -> p (n t)").bitcast(I32))
-        load_scale_rows(nc.scalar, xt_s, xt_scales)
+        nc.sync.dma_start(out=xt_w[:, : T // 2].bitcast(I32), in_=xt_rows[:, : T // 2])
+        load_scale_rows(nc.sync, xt_s, xt_scales)
+        nc.sync.dma_start(out=xt_w[:, T // 2 :].bitcast(I32), in_=xt_rows[:, T // 2 :])
         nc.sync.dma_start(fill_from[:], offs3)
         nc.sync.dma_start(out=sa_t[:], in_=sa.rearrange("(p t) o -> p (t o)", t=PACK))
         nc.sync.dma_start(fill_to[:], offs4)
@@ -84,47 +89,45 @@ def tile_picked_tokens_store_one_wholepage_further_plain_kernel(
 
         feat_s = keep.tile([P, R], U8, align_bytes=64)
         feat_w = keep.tile([P, R], U32, align_bytes=64)
-        slot_s = keep.tile([P, J], U8, align_bytes=64)
-        slot_w = [keep.tile([P, HALF_J], U32, align_bytes=64, name=f"slot_w{h}") for h in range(2)]
+        slot_s = keep.tile([P, J], U8, align_bytes=64, tag="token_bytes")
+        slot_w = keep.tile([P, J], U32, align_bytes=64, tag="token_words")
         nc.vector.tensor_copy(feat_s[:].rearrange("p (t m) -> p m t", t=PACK), wt_s[:].indirect(feature_list[:]))
         nc.vector.tensor_copy(feat_w[:].rearrange("p (t m) -> p m t", t=PACK), wt_w[:].indirect(feature_list[:]))
         nc.vector.tensor_copy(slot_s[:], xt_s[:].indirect(slot_list[:]))
-        for h in range(2):
-            nc.vector.tensor_copy(slot_w[h][:], xt_w[:].indirect(entries(slot_list, h * HALF_J, HALF_J)))
+        for first, count in SLOT_PIECES:
+            nc.vector.tensor_copy(slot_w[:, first : first + count], xt_w[:].indirect(entries(slot_list, first, count)))
 
         hidden = [keep.tile([P, J], F32, name=f"hidden{t}") for t in range(PACK)]
 
-        def first_product(acc, t, h):
+        def first_product(t, first, count, bank_tag):
+            bank = psum.tile([P, count], F32, name=f"first{t}_{first}", tag=bank_tag)
             nc.tensor.matmul_mx(
-                out=acc,
+                out=bank[:],
                 lhsT=feat_w[:, t * P : (t + 1) * P].bitcast(FP8X4),
                 lhsT_scale=feat_s[:, t * P : (t + 1) * P],
-                rhs=slot_w[h][:].bitcast(FP8X4),
-                rhs_scale=slot_s[:, h * HALF_J : (h + 1) * HALF_J],
+                rhs=slot_w[:, first : first + count].bitcast(FP8X4),
+                rhs_scale=slot_s[:, first : first + count],
                 start=True,
                 stop=True,
             )
+            return bank
 
-        for h in range(2):
-            bank = psum.tile([P, HALF_J], F32, name=f"lead{h}", tag=f"lead{h}")
-            first_product(bank[:], 0, h)
-            nc.scalar.copy(hidden[0][:, h * HALF_J : (h + 1) * HALF_J], bank[:])
+        for i, (first, count) in enumerate(SLOT_PIECES):
+            bank = first_product(0, first, count, f"first{i}")
+            nc.scalar.activation(hidden[0][:, first : first + count], bank[:], COPY)
         for t in range(1, PACK):
-            bank = psum.tile([P, J], F32, name=f"rest{t}", tag=f"rest{t}")
-            for h in range(2):
-                first_product(bank[:, h * HALF_J : (h + 1) * HALF_J], t, h)
+            bank = first_product(t, 0, J, f"first{t - 1}")
             nc.vector.tensor_copy(hidden[t][:], bank[:])
 
-        short_s = keep.tile([P, C], U8, align_bytes=64)
-        short_w = keep.tile([P, C], U32, align_bytes=64)
+        short_s = keep.tile([P, C], U8, align_bytes=64, tag="token_bytes")
+        short_w = keep.tile([P, C], U32, align_bytes=64, tag="token_words")
         nc.vector.tensor_copy(short_s[:], xt_s[:].indirect(short_list[:]))
         nc.vector.tensor_copy(short_w[:], xt_w[:].indirect(short_list[:]))
 
         sums = {}
         for h in range(2):
             for nt in range(2):
-                tag = "lead0" if (h, nt) == (1, 1) else f"sum{h}{nt}"
-                sums[h, nt] = psum.tile([P, HALF_C], F32, name=f"sum{h}{nt}", tag=tag)
+                sums[h, nt] = psum.tile([P, HALF_C], F32, name=f"sum{h}{nt}")
                 nc.tensor.matmul_mx(
                     out=sums[h, nt][:],
                     lhsT=ws_w[:, 2 * nt * P : 2 * (nt + 1) * P].bitcast(FP4X4),
@@ -135,34 +138,40 @@ def tile_picked_tokens_store_one_wholepage_further_plain_kernel(
                     stop=False,
                 )
 
-        fetched = [keep.tile([P, C], F32, name=f"fetched{t}") for t in range(PACK)]
-        filling = [keep.tile([P, O], F32, name=f"filling{t}") for t in range(PACK)]
-        diff = [keep.tile([P, C], F32, name=f"diff{t}") for t in range(PACK)]
-        hid = [keep.tile([P, HALF_C, PACK], BF16, align_bytes=64, name=f"hid{h}") for h in range(2)]
+        diff = keep.tile([P, PACK, C], F32)
+        hid = keep.tile([P, C, PACK], BF16, align_bytes=64)
+        halves = [slice(h * HALF_C, (h + 1) * HALF_C) for h in range(2)]
 
-        def fetch_filling(t):
-            nc.scalar.activation(filling[t][:], hidden[t][:].indirect(fill_from[:]), COPY, scale=sa_t[:, t : t + 1])
+        def difference(t, cols, fetched):
+            nc.vector.tensor_tensor(diff[:, t, cols], pages[t][:, cols], fetched[:, cols], ALU.subtract)
 
-        def fill_page(t):
-            nc.scalar.activation(pages[t][:].indirect(fill_to[:]), filling[t][:], COPY)
+        def pair_of_diff(t, cols):
+            return diff[:, t : t + 2, cols].rearrange("p t c -> p c t")
 
-        def fetch_columns(t, first, count):
-            nc.scalar.activation(
-                fetched[t][:, first : first + count],
-                hidden[t][:].indirect(entries(page_list, first, count)),
-                COPY,
-                scale=sb_t[:, t : t + 1],
-            )
+        def magnitude_on_vector(t, cols):
+            pair = pair_of_diff(t, cols)
+            nc.vector.scalar_tensor_tensor(hid[:, cols, t : t + 2], pair, -1.0, pair, ALU.mult, ALU.max)
 
-        def magnitude(t, h):
-            cols = slice(h * HALF_C, (h + 1) * HALF_C)
-            nc.vector.tensor_tensor(diff[t][:, cols], pages[t][:, cols], fetched[t][:, cols], ALU.subtract)
-            nc.vector.scalar_tensor_tensor(hid[h][:, :, t], diff[t][:, cols], -1.0, diff[t][:, cols], ALU.mult, ALU.max)
+        for t in range(PACK):
+            filling = keep.tile([P, O], F32, name=f"filling{t}", tag=f"lookup{t + 1}")
+            fetched = keep.tile([P, C], F32, name=f"fetched{t}", tag=f"lookup{t}")
+            nc.scalar.activation(filling[:], hidden[t][:].indirect(fill_from[:]), COPY, scale=sa_t[:, t : t + 1])
+            nc.scalar.activation(fetched[:], hidden[t][:].indirect(page_list[:]), COPY, scale=sb_t[:, t : t + 1])
+            nc.scalar.activation(pages[t][:].indirect(fill_to[:]), filling[:], COPY)
+            if t < PACK - 1:
+                difference(t, slice(0, C), fetched)
+            else:
+                for cols in halves:
+                    difference(t, cols, fetched)
+            if t == 1:
+                magnitude_on_vector(0, slice(0, C))
+        nc.scalar.activation(hid[:, halves[0], 2:4], pair_of_diff(2, halves[0]), ABS)
+        magnitude_on_vector(2, halves[1])
 
         def finish(h):
             codes = keep.tile([P, HALF_C], U32, align_bytes=64, name=f"codes{h}")
             scales = keep.tile([P, HALF_C], U8, align_bytes=64, name=f"scales{h}")
-            nc.vector.quantize_mx(out=codes[:].bitcast(FP8X4), scales=scales[:], in_=hid[h][:].rearrange("p c t -> p (c t)"))
+            nc.vector.quantize_mx(out=codes[:].bitcast(FP8X4), scales=scales[:], in_=hid[:, halves[h], :].rearrange("p c t -> p (c t)"))
             for nt in range(2):
                 nc.tensor.matmul_mx(
                     out=sums[h, nt][:],
@@ -177,26 +186,11 @@ def tile_picked_tokens_store_one_wholepage_further_plain_kernel(
                 result = keep.tile([P, HALF_C], F32, name=f"result{h}{nt}")
                 target = out[nt * P : (nt + 1) * P, h * HALF_C : (h + 1) * HALF_C]
                 if nt == 0:
-                    nc.scalar.copy(result[:], sums[h, nt][:])
+                    nc.scalar.activation(result[:], sums[h, nt][:], COPY)
                     nc.scalar.dma_start(out=target, in_=result[:])
                 else:
                     nc.vector.tensor_copy(result[:], sums[h, nt][:])
                     nc.sync.dma_start(out=target, in_=result[:])
 
-        for t in range(2):
-            fetch_filling(t)
-            fetch_columns(t, 0, C)
-            fill_page(t)
-            magnitude(t, 0)
-            magnitude(t, 1)
-        for t in range(2, PACK):
-            fetch_filling(t)
-            fetch_columns(t, 0, HALF_C)
-            fill_page(t)
-            magnitude(t, 0)
-        for t in range(2, PACK):
-            fetch_columns(t, HALF_C, HALF_C)
-        finish(0)
-        for t in range(2, PACK):
-            magnitude(t, 1)
-        finish(1)
+        for h in range(2):
+            finish(h)

@@ -70,14 +70,14 @@ def tile_picked_tokens_store_one_wholepage_further_plain_kernel(
 
         xt_rows = xt_words[0].rearrange("p n t -> p (n t)").bitcast(I32)
         nc.sync.dma_start(feature_list[:], offs2)
-        load_scale_rows(nc.sync, wt_s, wt_scales)
-        nc.sync.dma_start(slot_list[:], offs)
         nc.sync.dma_start(out=wt_w[:].bitcast(I32), in_=wt_words[0].rearrange("p n t -> p (n t)").bitcast(I32))
+        nc.sync.dma_start(slot_list[:], offs)
+        nc.sync.dma_start(out=sa_t[:], in_=sa.rearrange("(p t) o -> p (t o)", t=PACK))
+        load_scale_rows(nc.sync, wt_s, wt_scales)
         nc.sync.dma_start(out=xt_w[:, : T // 2].bitcast(I32), in_=xt_rows[:, : T // 2])
         load_scale_rows(nc.sync, xt_s, xt_scales)
         nc.sync.dma_start(out=xt_w[:, T // 2 :].bitcast(I32), in_=xt_rows[:, T // 2 :])
         nc.sync.dma_start(fill_from[:], offs3)
-        nc.sync.dma_start(out=sa_t[:], in_=sa.rearrange("(p t) o -> p (t o)", t=PACK))
         nc.sync.dma_start(fill_to[:], offs4)
         nc.sync.dma_start(page_list[:], offs5)
         nc.sync.dma_start(out=sb_t[:], in_=sb.rearrange("(p t) o -> p (t o)", t=PACK))
@@ -165,8 +165,8 @@ def tile_picked_tokens_store_one_wholepage_further_plain_kernel(
                     difference(t, cols, fetched)
             if t == 1:
                 magnitude_on_vector(0, slice(0, C))
-        nc.scalar.activation(hid[:, halves[0], 2:4], pair_of_diff(2, halves[0]), ABS)
-        magnitude_on_vector(2, halves[1])
+        for cols in halves:
+            nc.scalar.activation(hid[:, cols, 2:4], pair_of_diff(2, cols), ABS)
 
         def finish(h):
             codes = keep.tile([P, HALF_C], U32, align_bytes=64, name=f"codes{h}")

@@ -19,14 +19,18 @@ ALU = mybir.AluOpType
 
 P = 128
 PACK = 4
+QUADRANTS = 4
 LIST_ROWS = 16
 SLOT_PIECES = ((0, 256), (256, 128), (384, 128))
 HALF_C = C // 2
 
 
-def load_scale_rows(queue, plane, scales):
-    for q in range(4):
-        queue.dma_start(out=plane[32 * q : 32 * q + 4, :].bitcast(I32), in_=scales[0, 4 * q : 4 * q + 4, :].bitcast(I32))
+def load_scale_rows(nc, plane, scales):
+    for q in range(QUADRANTS):
+        nc.sync.dma_start(
+            out=plane[32 * q : 32 * q + 4, :].bitcast(I32),
+            in_=scales[0, 4 * q : 4 * q + 4, :].bitcast(I32),
+        )
 
 
 def entries(offsets, first, count):
@@ -73,9 +77,9 @@ def tile_picked_tokens_store_one_wholepage_further_plain_kernel(
         nc.sync.dma_start(out=wt_w[:].bitcast(I32), in_=wt_words[0].rearrange("p n t -> p (n t)").bitcast(I32))
         nc.sync.dma_start(slot_list[:], offs)
         nc.sync.dma_start(out=sa_t[:], in_=sa.rearrange("(p t) o -> p (t o)", t=PACK))
-        load_scale_rows(nc.sync, wt_s, wt_scales)
+        load_scale_rows(nc, wt_s, wt_scales)
         nc.sync.dma_start(out=xt_w[:, : T // 2].bitcast(I32), in_=xt_rows[:, : T // 2])
-        load_scale_rows(nc.sync, xt_s, xt_scales)
+        load_scale_rows(nc, xt_s, xt_scales)
         nc.sync.dma_start(out=xt_w[:, T // 2 :].bitcast(I32), in_=xt_rows[:, T // 2 :])
         nc.sync.dma_start(fill_from[:], offs3)
         nc.sync.dma_start(fill_to[:], offs4)
@@ -84,8 +88,8 @@ def tile_picked_tokens_store_one_wholepage_further_plain_kernel(
         nc.sync.dma_start(short_list[:], offs6)
         nc.sync.dma_start(out=ws_w[:].bitcast(I32), in_=ws_words[0].bitcast(I32))
         nc.sync.dma_start(out=wb_w[:].bitcast(I32), in_=wb_words[0].bitcast(I32))
-        load_scale_rows(nc.sync, ws_s, ws_scales)
-        load_scale_rows(nc.sync, wb_s, wb_scales)
+        load_scale_rows(nc, ws_s, ws_scales)
+        load_scale_rows(nc, wb_s, wb_scales)
 
         feat_s = keep.tile([P, R], U8, align_bytes=64)
         feat_w = keep.tile([P, R], U32, align_bytes=64)
@@ -124,73 +128,74 @@ def tile_picked_tokens_store_one_wholepage_further_plain_kernel(
         nc.vector.tensor_copy(short_s[:], xt_s[:].indirect(short_list[:]))
         nc.vector.tensor_copy(short_w[:], xt_w[:].indirect(short_list[:]))
 
+        halves = [slice(h * HALF_C, (h + 1) * HALF_C) for h in range(2)]
         sums = {}
         for h in range(2):
-            for nt in range(2):
+            for nt in range(N // P):
                 sums[h, nt] = psum.tile([P, HALF_C], F32, name=f"sum{h}{nt}")
                 nc.tensor.matmul_mx(
                     out=sums[h, nt][:],
                     lhsT=ws_w[:, 2 * nt * P : 2 * (nt + 1) * P].bitcast(FP4X4),
                     lhsT_scale=ws_s[:, nt * P : (nt + 1) * P],
-                    rhs=short_w[:, h * HALF_C : (h + 1) * HALF_C].bitcast(FP8X4),
-                    rhs_scale=short_s[:, h * HALF_C : (h + 1) * HALF_C],
+                    rhs=short_w[:, halves[h]].bitcast(FP8X4),
+                    rhs_scale=short_s[:, halves[h]],
                     start=True,
                     stop=False,
                 )
 
         diff = keep.tile([P, PACK, C], F32)
         hid = keep.tile([P, C, PACK], BF16, align_bytes=64)
-        halves = [slice(h * HALF_C, (h + 1) * HALF_C) for h in range(2)]
+
+        def fetch_columns(t, cols, tag):
+            count = cols.stop - cols.start
+            fetched = keep.tile([P, count], F32, name=f"fetched{t}_{cols.start}", tag=tag)
+            listed = hidden[t][:].indirect(entries(page_list, cols.start, count))
+            nc.scalar.activation(fetched[:], listed, COPY, scale=sb_t[:, t : t + 1])
+            return fetched
 
         def difference(t, cols, fetched):
-            nc.vector.tensor_tensor(diff[:, t, cols], pages[t][:, cols], fetched[:, cols], ALU.subtract)
+            nc.vector.tensor_tensor(diff[:, t, cols], pages[t][:, cols], fetched[:], ALU.subtract)
 
         def pair_of_diff(t, cols):
             return diff[:, t : t + 2, cols].rearrange("p t c -> p c t")
 
-        def magnitude_on_vector(t, cols):
-            pair = pair_of_diff(t, cols)
-            nc.vector.scalar_tensor_tensor(hid[:, cols, t : t + 2], pair, -1.0, pair, ALU.mult, ALU.max)
-
+        last = PACK - 1
+        whole = slice(0, C)
         for t in range(PACK):
+            cols = halves[0] if t == last else whole
             filling = keep.tile([P, O], F32, name=f"filling{t}", tag=f"lookup{t + 1}")
-            fetched = keep.tile([P, C], F32, name=f"fetched{t}", tag=f"lookup{t}")
             nc.scalar.activation(filling[:], hidden[t][:].indirect(fill_from[:]), COPY, scale=sa_t[:, t : t + 1])
-            nc.scalar.activation(fetched[:], hidden[t][:].indirect(page_list[:]), COPY, scale=sb_t[:, t : t + 1])
+            fetched = fetch_columns(t, cols, f"lookup{t}")
             nc.scalar.activation(pages[t][:].indirect(fill_to[:]), filling[:], COPY)
-            if t < PACK - 1:
-                difference(t, slice(0, C), fetched)
-            else:
-                for cols in halves:
-                    difference(t, cols, fetched)
+            difference(t, cols, fetched)
             if t == 1:
-                magnitude_on_vector(0, slice(0, C))
+                pair = pair_of_diff(0, whole)
+                nc.vector.scalar_tensor_tensor(hid[:, :, 0:2], pair, -1.0, pair, ALU.mult, ALU.max)
+        difference(last, halves[1], fetch_columns(last, halves[1], f"lookup{PACK}"))
         for cols in halves:
             nc.scalar.activation(hid[:, cols, 2:4], pair_of_diff(2, cols), ABS)
 
-        def finish(h):
+        for h in range(2):
             codes = keep.tile([P, HALF_C], U32, align_bytes=64, name=f"codes{h}")
-            scales = keep.tile([P, HALF_C], U8, align_bytes=64, name=f"scales{h}")
-            nc.vector.quantize_mx(out=codes[:].bitcast(FP8X4), scales=scales[:], in_=hid[:, halves[h], :].rearrange("p c t -> p (c t)"))
-            for nt in range(2):
+            code_scales = keep.tile([P, HALF_C], U8, align_bytes=64, name=f"scales{h}")
+            nc.vector.quantize_mx(
+                out=codes[:].bitcast(FP8X4),
+                scales=code_scales[:],
+                in_=hid[:, halves[h], :].rearrange("p c t -> p (c t)"),
+            )
+            for nt in range(N // P):
                 nc.tensor.matmul_mx(
                     out=sums[h, nt][:],
                     lhsT=wb_w[:, 2 * nt * P : 2 * (nt + 1) * P].bitcast(FP4X4),
                     lhsT_scale=wb_s[:, nt * P : (nt + 1) * P],
                     rhs=codes[:].bitcast(FP8X4),
-                    rhs_scale=scales[:],
+                    rhs_scale=code_scales[:],
                     start=False,
                     stop=True,
                 )
-            for nt in range(2):
-                result = keep.tile([P, HALF_C], F32, name=f"result{h}{nt}")
-                target = out[nt * P : (nt + 1) * P, h * HALF_C : (h + 1) * HALF_C]
-                if nt == 0:
-                    nc.scalar.activation(result[:], sums[h, nt][:], COPY)
-                    nc.scalar.dma_start(out=target, in_=result[:])
-                else:
-                    nc.vector.tensor_copy(result[:], sums[h, nt][:])
-                    nc.sync.dma_start(out=target, in_=result[:])
-
-        for h in range(2):
-            finish(h)
+            upper = keep.tile([P, HALF_C], F32, name=f"result{h}0")
+            nc.scalar.activation(upper[:], sums[h, 0][:], COPY)
+            nc.scalar.dma_start(out=out[:P, halves[h]], in_=upper[:])
+            lower = keep.tile([P, HALF_C], F32, name=f"result{h}1")
+            nc.vector.tensor_copy(lower[:], sums[h, 1][:])
+            nc.sync.dma_start(out=out[P:, halves[h]], in_=lower[:])

from contextlib import ExitStack

import concourse.mybir as mybir

K, J, R, T, F, O, C, N = 512, 512, 512, 2048, 1024, 192, 256, 256
FLOPS = 2 * K * R * J + 2 * R * N * C + 2 * K * N * C

F32 = mybir.dt.float32
BF16 = mybir.dt.bfloat16
I32 = mybir.dt.int32
U32 = mybir.dt.uint32
U16 = mybir.dt.uint16
U8 = mybir.dt.uint8
FP8X4 = mybir.dt.float8_e4m3fn_x4
FP4X4 = mybir.dt.float4_e2m1fn_x4
COPY = mybir.ActivationFunctionType.Copy
ABS = mybir.ActivationFunctionType.Abs
ALU = mybir.AluOpType

P = 128
PACK = 4
QUADRANTS = 4
LIST_ROWS = 16
SLOT_PIECES = ((0, 256), (256, 128), (384, 128))
HALF_C = C // 2


def load_scale_rows(nc, plane, scales):
    for q in range(QUADRANTS):
        nc.sync.dma_start(
            out=plane[32 * q : 32 * q + 4, :].bitcast(I32),
            in_=scales[0, 4 * q : 4 * q + 4, :].bitcast(I32),
        )


def entries(offsets, first, count):
    return offsets[:, first // LIST_ROWS : (first + count) // LIST_ROWS]


def tile_picked_tokens_store_one_wholepage_further_plain_kernel(
    tc, xt_words, xt_scales, wt_words, wt_scales, sa, sb, wb_words, wb_scales, ws_words, ws_scales,
    offs, offs2, offs3, offs4, offs5, offs6, out,
):
    nc = tc.nc
    with ExitStack() as ctx:
        keep = ctx.enter_context(tc.tile_pool(name="keep", bufs=1))
        psum = ctx.enter_context(tc.psum_pool(name="psum", bufs=1))

        slot_list = keep.tile([P, J // LIST_ROWS], U16)
        feature_list = keep.tile([P, R // LIST_ROWS], U16)
        fill_from = keep.tile([P, O // LIST_ROWS], U16)
        fill_to = keep.tile([P, O // LIST_ROWS], U16)
        page_list = keep.tile([P, C // LIST_ROWS], U16)
        short_list = keep.tile([P, C // LIST_ROWS], U16)

        xt_w = keep.tile([P, T], U32, align_bytes=64)
        xt_s = keep.tile([P, T], U8, align_bytes=64)
        wt_w = keep.tile([P, F], U32, align_bytes=64)
        wt_s = keep.tile([P, F], U8, align_bytes=64)
        wb_w = keep.tile([P, 2 * N], U8, align_bytes=64)
        wb_s = keep.tile([P, N], U8, align_bytes=64)
        ws_w = keep.tile([P, 2 * N], U8, align_bytes=64)
        ws_s = keep.tile([P, N], U8, align_bytes=64)
        sa_t = keep.tile([P, PACK], F32)
        sb_t = keep.tile([P, PACK], F32)
        pages = [keep.tile([P, C], F32, name=f"page{t}") for t in range(PACK)]

        for plane in (wt_s, xt_s):
            nc.vector.memset(plane[:].bitcast(I32), 0)
        for page in pages:
            nc.vector.memset(page[:], 0.0)
        for plane in (ws_s, wb_s):
            nc.vector.memset(plane[:].bitcast(I32), 0)

        xt_rows = xt_words[0].rearrange("p n t -> p (n t)").bitcast(I32)
        nc.sync.dma_start(feature_list[:], offs2)
        nc.sync.dma_start(out=wt_w[:].bitcast(I32), in_=wt_words[0].rearrange("p n t -> p (n t)").bitcast(I32))
        nc.sync.dma_start(slot_list[:], offs)
        nc.sync.dma_start(out=sa_t[:], in_=sa.rearrange("(p t) o -> p (t o)", t=PACK))
        load_scale_rows(nc, wt_s, wt_scales)
        nc.sync.dma_start(out=xt_w[:, : T // 2].bitcast(I32), in_=xt_rows[:, : T // 2])
        load_scale_rows(nc, xt_s, xt_scales)
        nc.sync.dma_start(out=xt_w[:, T // 2 :].bitcast(I32), in_=xt_rows[:, T // 2 :])
        nc.sync.dma_start(fill_from[:], offs3)
        nc.sync.dma_start(fill_to[:], offs4)
        nc.sync.dma_start(page_list[:], offs5)
        nc.sync.dma_start(out=sb_t[:], in_=sb.rearrange("(p t) o -> p (t o)", t=PACK))
        nc.sync.dma_start(short_list[:], offs6)
        nc.sync.dma_start(out=ws_w[:].bitcast(I32), in_=ws_words[0].bitcast(I32))
        nc.sync.dma_start(out=wb_w[:].bitcast(I32), in_=wb_words[0].bitcast(I32))
        load_scale_rows(nc, ws_s, ws_scales)
        load_scale_rows(nc, wb_s, wb_scales)

        feat_s = keep.tile([P, R], U8, align_bytes=64)
        feat_w = keep.tile([P, R], U32, align_bytes=64)
        slot_s = keep.tile([P, J], U8, align_bytes=64, tag="token_bytes")
        slot_w = keep.tile([P, J], U32, align_bytes=64, tag="token_words")
        nc.vector.tensor_copy(feat_s[:].rearrange("p (t m) -> p m t", t=PACK), wt_s[:].indirect(feature_list[:]))
        nc.vector.tensor_copy(feat_w[:].rearrange("p (t m) -> p m t", t=PACK), wt_w[:].indirect(feature_list[:]))
        nc.vector.tensor_copy(slot_s[:], xt_s[:].indirect(slot_list[:]))
        for first, count in SLOT_PIECES:
            nc.vector.tensor_copy(slot_w[:, first : first + count], xt_w[:].indirect(entries(slot_list, first, count)))

        hidden = [keep.tile([P, J], F32, name=f"hidden{t}") for t in range(PACK)]

        def first_product(t, first, count, bank_tag):
            bank = psum.tile([P, count], F32, name=f"first{t}_{first}", tag=bank_tag)
            nc.tensor.matmul_mx(
                out=bank[:],
                lhsT=feat_w[:, t * P : (t + 1) * P].bitcast(FP8X4),
                lhsT_scale=feat_s[:, t * P : (t + 1) * P],
                rhs=slot_w[:, first : first + count].bitcast(FP8X4),
                rhs_scale=slot_s[:, first : first + count],
                start=True,
                stop=True,
            )
            return bank

        for i, (first, count) in enumerate(SLOT_PIECES):
            bank = first_product(0, first, count, f"first{i}")
            nc.scalar.activation(hidden[0][:, first : first + count], bank[:], COPY)
        for t in range(1, PACK):
            bank = first_product(t, 0, J, f"first{t - 1}")
            nc.vector.tensor_copy(hidden[t][:], bank[:])

        short_s = keep.tile([P, C], U8, align_bytes=64, tag="token_bytes")
        short_w = keep.tile([P, C], U32, align_bytes=64, tag="token_words")
        nc.vector.tensor_copy(short_s[:], xt_s[:].indirect(short_list[:]))
        nc.vector.tensor_copy(short_w[:], xt_w[:].indirect(short_list[:]))

        halves = [slice(h * HALF_C, (h + 1) * HALF_C) for h in range(2)]
        sums = {}
        for h in range(2):
            for nt in range(N // P):
                sums[h, nt] = psum.tile([P, HALF_C], F32, name=f"sum{h}{nt}")
                nc.tensor.matmul_mx(
                    out=sums[h, nt][:],
                    lhsT=ws_w[:, 2 * nt * P : 2 * (nt + 1) * P].bitcast(FP4X4),
                    lhsT_scale=ws_s[:, nt * P : (nt + 1) * P],
                    rhs=short_w[:, halves[h]].bitcast(FP8X4),
                    rhs_scale=short_s[:, halves[h]],
                    start=True,
                    stop=False,
                )

        diff = keep.tile([P, PACK, C], F32)
        hid = keep.tile([P, C, PACK], BF16, align_bytes=64)

        def fetch_columns(t, cols, tag):
            count = cols.stop - cols.start
            fetched = keep.tile([P, count], F32, name=f"fetched{t}_{cols.start}", tag=tag)
            listed = hidden[t][:].indirect(entries(page_list, cols.start, count))
            nc.scalar.activation(fetched[:], listed, COPY, scale=sb_t[:, t : t + 1])
            return fetched

        def difference(t, cols, fetched):
            nc.vector.tensor_tensor(diff[:, t, cols], pages[t][:, cols], fetched[:], ALU.subtract)

        def pair_of_diff(t, cols):
            return diff[:, t : t + 2, cols].rearrange("p t c -> p c t")

        last = PACK - 1
        whole = slice(0, C)
        for t in range(PACK):
            cols = halves[0] if t == last else whole
            filling = keep.tile([P, O], F32, name=f"filling{t}", tag=f"lookup{t + 1}")
            nc.scalar.activation(filling[:], hidden[t][:].indirect(fill_from[:]), COPY, scale=sa_t[:, t : t + 1])
            fetched = fetch_columns(t, cols, f"lookup{t}")
            nc.scalar.activation(pages[t][:].indirect(fill_to[:]), filling[:], COPY)
            difference(t, cols, fetched)
            if t == 1:
                pair = pair_of_diff(0, whole)
                nc.vector.scalar_tensor_tensor(hid[:, :, 0:2], pair, -1.0, pair, ALU.mult, ALU.max)
        difference(last, halves[1], fetch_columns(last, halves[1], f"lookup{PACK}"))
        for cols in halves:
            nc.scalar.activation(hid[:, cols, 2:4], pair_of_diff(2, cols), ABS)

        for h in range(2):
            codes = keep.tile([P, HALF_C], U32, align_bytes=64, name=f"codes{h}")
            code_scales = keep.tile([P, HALF_C], U8, align_bytes=64, name=f"scales{h}")
            nc.vector.quantize_mx(
                out=codes[:].bitcast(FP8X4),
                scales=code_scales[:],
                in_=hid[:, halves[h], :].rearrange("p c t -> p (c t)"),
            )
            for nt in range(N // P):
                nc.tensor.matmul_mx(
                    out=sums[h, nt][:],
                    lhsT=wb_w[:, 2 * nt * P : 2 * (nt + 1) * P].bitcast(FP4X4),
                    lhsT_scale=wb_s[:, nt * P : (nt + 1) * P],
                    rhs=codes[:].bitcast(FP8X4),
                    rhs_scale=code_scales[:],
                    start=False,
                    stop=True,
                )
            upper = keep.tile([P, HALF_C], F32, name=f"result{h}0")
            nc.scalar.activation(upper[:], sums[h, 0][:], COPY)
            nc.scalar.dma_start(out=out[:P, halves[h]], in_=upper[:])
            lower = keep.tile([P, HALF_C], F32, name=f"result{h}1")
            nc.vector.tensor_copy(lower[:], sums[h, 1][:])
            nc.sync.dma_start(out=out[P:, halves[h]], in_=lower[:])
